import numpy as np
import ml_dtypes


def mxq(x, axis, fmt="e4m3"):
    dtype, down = {"e4m3": (ml_dtypes.float8_e4m3fn, 7), "e5m2": (ml_dtypes.float8_e5m2, 14)}[fmt]
    v = np.moveaxis(np.asarray(x, np.float32).astype(ml_dtypes.bfloat16).astype(np.float64), axis, -1)
    blocks = v.reshape(v.shape[:-1] + (-1, 32))
    amax = np.abs(blocks).max(-1, keepdims=True)
    byte = np.maximum(np.where(amax > 0, np.frexp(amax)[1] - 1 + 127, 0) - down, 1)
    scale = np.exp2(byte - 127.0)
    codes = (blocks / scale).astype(np.float32).astype(dtype).astype(np.float64)
    return np.moveaxis((codes * scale).reshape(v.shape), -1, axis)


WIDE = False


def mx_kscale(k):
    if not WIDE:
        return np.ones(k)
    levels = np.array([10, -10, 5, -5, 0])
    if k % 512:
        return np.exp2(np.random.permutation(np.resize(levels, k // 32))).repeat(32)
    a = np.empty((k // 512, 16))
    for p in range(k // 512):
        a[p, :8] = np.random.permutation(np.resize(levels, 8))
        for g in range(8):
            far = levels[np.abs(levels - a[p, g]) >= 10]
            a[p, g + 8] = far[np.random.randint(len(far))]
    return np.exp2(a.ravel()).repeat(32)


def f64(x):
    return np.asarray(x).astype(np.float64)


def striped(idx):
    return np.tile(np.asarray(idx).reshape(-1, 16).T, (8, 1)).astype(np.uint16)


def unstriped(offs):
    return offs[:16].T.reshape(-1).astype(np.int64)


def striped8(idx):
    return np.asarray(idx).reshape(8, -1, 16).transpose(0, 2, 1).reshape(128, -1).astype(np.uint16)


def unstriped8(offs):
    return offs.reshape(8, 16, -1).transpose(0, 2, 1).reshape(8, -1).astype(np.int64)


def pick8(x, idx, run):
    r = np.arange(len(x))
    return x[r[:, None], idx[r % (8 * run) // run]]


E2M1 = np.array([0.0, 0.5, 1.0, 1.5, 2.0, 3.0, 4.0, 6.0, -0.0, -0.5, -1.0, -1.5, -2.0, -3.0, -4.0, -6.0])


def pack_weight(w, fmt):
    k, n = w.shape
    w = f64(np.asarray(w, np.float32).astype(ml_dtypes.bfloat16)).reshape(k // 32, 32, n)
    amax = np.abs(w).max(1)
    if fmt == "e4m3":
        byte = np.frexp(amax)[1] - 1 + 127 - 7
    else:
        mant, ex = np.frexp(amax / 6.0)
        byte = np.where(mant > 0.5, ex, ex - 1) + 127
    byte = np.clip(np.where(amax > 0, byte, 1), 1, 254)
    scaled = (w * np.exp2(127.0 - byte)[:, None, :]).reshape(k, n).astype(np.float32)
    by_word = np.ascontiguousarray(scaled.reshape(k // 512, 128, 4, n).transpose(0, 1, 3, 2))
    if fmt == "e4m3":
        words = by_word.astype(ml_dtypes.float8_e4m3fn).view(np.uint8)
    else:
        c = by_word.astype(ml_dtypes.float4_e2m1fn).view(np.uint8) & 0xF
        words = (c[..., 0::2] | (c[..., 1::2] << 4)).reshape(k // 512, 128, 2 * n)
    return np.ascontiguousarray(words), np.ascontiguousarray(byte.astype(np.uint8).reshape(k // 512, 16, n))


def unpack_weight(words, scales, fmt):
    g, _, n = scales.shape
    words = np.ascontiguousarray(words).reshape(g, 128, n, -1)
    if fmt == "e4m3":
        vals = words.view(ml_dtypes.float8_e4m3fn).astype(np.float64)
    else:
        nib = np.empty((g, 128, n, 4), np.uint8)
        nib[..., 0::2] = words & 0xF
        nib[..., 1::2] = words >> 4
        vals = E2M1[nib]
    vals = vals * np.repeat(np.exp2(scales.astype(np.float64) - 127.0), 8, axis=1)[..., None]
    return vals.transpose(0, 1, 3, 2).reshape(g * 512, n)


def sigmoid(v):
    return 1.0 / (1.0 + np.exp(-v))


K, R, F, T, J, M = 512, 128, 512, 2048, 512, 256


def setup_inputs():
    n = np.random.standard_normal
    idx = np.random.permutation(T)[:J]
    idx4 = np.random.permutation(T)[:J]
    idx2 = np.stack([np.random.permutation(J)[:M] for _ in range(8)])
    idx3 = np.stack([np.random.permutation(J)[:M] for _ in range(8)])
    fk = mx_kscale(K)
    ff = mx_kscale(F)
    tabp = pack_weight(n((K, T)) / fk[:, None], "e2m1")
    tab2p = pack_weight(n((K, T)) / fk[:, None], "e2m1")
    return {
        "tab_words": tabp[0],
        "tab_scales": tabp[1],
        "w1": (n((K, R)) * 1 / np.sqrt(K) * fk[:, None]).astype(np.float32),
        "tab2_words": tab2p[0],
        "tab2_scales": tab2p[1],
        "w2": (n((K, R)) * 1 / np.sqrt(K) * fk[:, None]).astype(np.float32),
        "gain": (np.random.uniform(0.5, 1.5, (R, 1))).astype(np.float32),
        "wo": (n((F, R)) * 1 / np.sqrt(F) * ff[:, None]).astype(np.float32),
        "dy": (n((F, M)) / ff[:, None]).astype(np.float32),
        "old": (0.5 * n((R, J))).astype(np.float32),
        "offs": striped(idx),
        "offs4": striped(idx4),
        "offs2": striped8(idx2),
        "offs3": striped8(idx3),
    }


def reference(tab_words, tab_scales, w1, tab2_words, tab2_scales, w2, gain, wo, dy, old, offs, offs4, offs2, offs3):
    idx = unstriped(offs)
    idx4 = unstriped(offs4)
    idx2 = unstriped8(offs2)
    idx3 = unstriped8(offs3)
    tabu = unpack_weight(tab_words, tab_scales, "e2m1")
    tab2u = unpack_weight(tab2_words, tab2_scales, "e2m1")
    w1q = mxq(f64(w1), 0, "e4m3")
    tabidxg = tabu[:, idx]
    a = w1q.T @ tabidxg
    w2q = mxq(f64(w2), 0, "e4m3")
    tab2idx4g = tab2u[:, idx4]
    b = w2q.T @ tab2idx4g
    h0 = np.tanh(a)
    g1 = sigmoid(b)
    woq = mxq(f64(wo), 0, "e4m3")
    dyq = mxq(f64(dy), 0, "e4m3")
    c0 = woq.T @ dyq
    e1 = c0 * pick8(g1, idx3, 16)
    s1 = np.zeros((R, J))
    s1[np.arange(R)[:, None], idx2[np.arange(R) % 128 // 16]] = e1
    dh0 = s1 * f64(gain)
    da = dh0 * (1.0 - np.square(h0))
    y = da + f64(old)
    return y

@@ -1,0 +1,139 @@
+from contextlib import ExitStack
+
+import concourse.mybir as mybir
+
+K, R, F, T, J, M = 512, 128, 512, 2048, 512, 256
+FLOPS = 2 * K * R * J * 2 + 2 * F * R * M
+
+F32 = mybir.dt.float32
+BF16 = mybir.dt.bfloat16
+I32 = mybir.dt.int32
+U32 = mybir.dt.uint32
+U16 = mybir.dt.uint16
+U8 = mybir.dt.uint8
+FP8X4 = mybir.dt.float8_e4m3fn_x4
+FP4X4 = mybir.dt.float4_e2m1fn_x4
+ACT = mybir.ActivationFunctionType
+ALU = mybir.AluOpType
+
+P = 128
+PACK = 4
+LINE = 4
+HALVES = 2
+
+
+def tile_attend_cpickgates_kernel(tc, tab_words, tab_scales, w1, tab2_words, tab2_scales, w2, gain, wo, dy, old,
+                                   offs, offs4, offs2, offs3, out):
+    nc = tc.nc
+    with ExitStack() as ctx:
+        sb = ctx.enter_context(tc.tile_pool(name="sb", bufs=1))
+        ps = ctx.enter_context(tc.psum_pool(name="ps", bufs=1))
+
+        def new(name, shape, dtype):
+            return sb.tile(shape, dtype, name=name, align_bytes=64)
+
+        def load_list(name, src):
+            t = new(name, list(src.shape), U16)
+            nc.sync.dma_start(t[:], src)
+            return t
+
+        def load_words(name, src):
+            t = new(name, [P, T], U16)
+            nc.sync.dma_start(t[:].bitcast(I32), src[0].bitcast(I32))
+            return t
+
+        def zeroed_plane(name):
+            t = new(name, [P, T], U8)
+            nc.vector.memset(t[:].bitcast(I32), 0)
+            return t
+
+        def load_scales(t, src):
+            rows = src[0].bitcast(I32).rearrange("(q r) c -> r q c", r=4)
+            for r in range(4):
+                nc.sync.dma_start(t[r:P:32, :].bitcast(I32), rows[r])
+
+        def load_rows(name, src):
+            t = new(name, [P, PACK, src.shape[1]], F32)
+            nc.sync.dma_start(t[:], src.rearrange("(p t) c -> p t c", t=PACK))
+            return t
+
+        def interleave(name, raw):
+            width = raw.shape[2]
+            t = new(name, [P, width * PACK], BF16)
+            nc.scalar.copy(t[:].rearrange("p (c i t) -> p c t i", i=LINE, t=PACK),
+                           raw[:].rearrange("p t (c i) -> p c t i", i=LINE))
+            return t
+
+        def quantise(name, grouped):
+            width = grouped.shape[1] // PACK
+            codes = new(name + "_codes", [P, width], U32)
+            plane = new(name + "_plane", [P, width], U8)
+            nc.vector.quantize_mx(codes[:].bitcast(FP8X4), plane[:], grouped[:])
+            return codes, plane
+
+        def gather(name, window, offsets, count, dtype):
+            t = new(name, [P, count], dtype)
+            nc.vector.tensor_copy(t[:], window[:].indirect(offsets[:]))
+            return t
+
+        def product(name, lhs, rhs, rhs_dtype):
+            acc = ps.tile([P, rhs[0].shape[1]], F32, name=name)
+            nc.tensor.matmul_mx(acc[:], lhsT=lhs[0][:].bitcast(FP8X4), lhsT_scale=lhs[1][:],
+                                rhs=rhs[0][:].bitcast(rhs_dtype), rhs_scale=rhs[1][:], start=True, stop=True)
+            return acc
+
+        plane2 = zeroed_plane("plane2")
+        plane1 = zeroed_plane("plane1")
+        placed = new("placed", [P, J], F32)
+        nc.vector.memset(placed[:], 0.0)
+
+        warm = new("warm", [P, 1], F32)
+        nc.scalar.activation(warm[:], placed[:, 0:1], ACT.Sigmoid)
+
+        words2 = load_words("words2", tab2_words)
+        list4 = load_list("list4", offs4)
+        load_scales(plane2, tab2_scales)
+        w2_raw = load_rows("w2_raw", w2)
+        words1 = load_words("words1", tab_words)
+        list1 = load_list("list1", offs)
+        load_scales(plane1, tab_scales)
+        wo_raw = load_rows("wo_raw", wo)
+        dy_raw = load_rows("dy_raw", dy)
+        w1_raw = load_rows("w1_raw", w1)
+        gain_col = new("gain_col", [P, 1], F32)
+        nc.sync.dma_start(gain_col[:], gain)
+        list3 = load_list("list3", offs3)
+        list2 = load_list("list2", offs2)
+        old_sb = new("old_sb", [P, J], F32)
+        nc.sync.dma_start(old_sb[:], old)
+
+        picked2 = (gather("picked2_words", words2, list4, J, U16), gather("picked2_plane", plane2, list4, J, U8))
+        w2_mx = quantise("w2", interleave("w2_bf", w2_raw))
+        b_acc = product("b_acc", w2_mx, picked2, FP4X4)
+        picked1 = (gather("picked1_words", words1, list1, J, U16), gather("picked1_plane", plane1, list1, J, U8))
+        gate = new("gate", [P, J], F32)
+        nc.scalar.activation(gate[:], b_acc[:], ACT.Sigmoid)
+        wo_mx = quantise("wo", interleave("wo_bf", wo_raw))
+        dy_mx = quantise("dy", interleave("dy_bf", dy_raw))
+        c_acc = product("c_acc", wo_mx, dy_mx, FP8X4)
+        w1_mx = quantise("w1", interleave("w1_bf", w1_raw))
+        a_acc = product("a_acc", w1_mx, picked1, FP4X4)
+        gate_picked = gather("gate_picked", gate, list3, M, F32)
+        c_gain = new("c_gain", [P, M], F32)
+        nc.scalar.activation(c_gain[:], c_acc[:], ACT.Copy, scale=gain_col[:])
+        nc.vector.tensor_tensor(placed[:].indirect(list2[:]), gate_picked[:], c_gain[:], ALU.mult)
+        hidden = new("hidden", [P, J], F32)
+        nc.scalar.activation(hidden[:], a_acc[:], ACT.Tanh)
+        squared = new("squared", [P, J], F32)
+        nc.scalar.activation(squared[:], hidden[:], ACT.Square)
+
+        width = J // HALVES
+        cols = [slice(h * width, (h + 1) * width) for h in range(HALVES)]
+        neg = [new("neg%d" % h, [P, width], F32) for h in range(HALVES)]
+        res = [new("res%d" % h, [P, width], F32) for h in range(HALVES)]
+        for h in range(HALVES):
+            nc.vector.scalar_tensor_tensor(neg[h][:], squared[:, cols[h]], 1.0, placed[:, cols[h]],
+                                           ALU.subtract, ALU.mult)
+        for h in range(HALVES):
+            nc.vector.tensor_tensor(res[h][:], old_sb[:, cols[h]], neg[h][:], ALU.subtract)
+            nc.sync.dma_start(out[:, cols[h]], res[h][:])

@@ -29,8 +29,8 @@ def tile_attend_cpickgates_kernel(tc, tab_words, tab_scales, w1, tab2_words, tab
         sb = ctx.enter_context(tc.tile_pool(name="sb", bufs=1))
         ps = ctx.enter_context(tc.psum_pool(name="ps", bufs=1))
 
-        def new(name, shape, dtype):
-            return sb.tile(shape, dtype, name=name, align_bytes=64)
+        def new(name, shape, dtype, tag=None):
+            return sb.tile(shape, dtype, name=name, tag=tag or name, align_bytes=64)
 
         def load_list(name, src):
             t = new(name, list(src.shape), U16)
@@ -64,9 +64,9 @@ def tile_attend_cpickgates_kernel(tc, tab_words, tab_scales, w1, tab2_words, tab
                            raw[:].rearrange("p t (c i) -> p c t i", i=LINE))
             return t
 
-        def quantise(name, grouped):
+        def quantise(name, grouped, tag=None):
             width = grouped.shape[1] // PACK
-            codes = new(name + "_codes", [P, width], U32)
+            codes = new(name + "_codes", [P, width], U32, tag)
             plane = new(name + "_plane", [P, width], U8)
             nc.vector.quantize_mx(codes[:].bitcast(FP8X4), plane[:], grouped[:])
             return codes, plane
@@ -93,35 +93,36 @@ def tile_attend_cpickgates_kernel(tc, tab_words, tab_scales, w1, tab2_words, tab
         words2 = load_words("words2", tab2_words)
         list4 = load_list("list4", offs4)
         load_scales(plane2, tab2_scales)
-        w2_raw = load_rows("w2_raw", w2)
+        dy_raw = load_rows("dy_raw", dy)
         words1 = load_words("words1", tab_words)
         list1 = load_list("list1", offs)
-        load_scales(plane1, tab_scales)
+        w2_raw = load_rows("w2_raw", w2)
         wo_raw = load_rows("wo_raw", wo)
-        dy_raw = load_rows("dy_raw", dy)
         w1_raw = load_rows("w1_raw", w1)
-        gain_col = new("gain_col", [P, 1], F32)
-        nc.sync.dma_start(gain_col[:], gain)
+        load_scales(plane1, tab_scales)
         list3 = load_list("list3", offs3)
         list2 = load_list("list2", offs2)
+        gain_col = new("gain_col", [P, 1], F32)
+        nc.sync.dma_start(gain_col[:], gain)
         old_sb = new("old_sb", [P, J], F32)
         nc.sync.dma_start(old_sb[:], old)
 
         picked2 = (gather("picked2_words", words2, list4, J, U16), gather("picked2_plane", plane2, list4, J, U8))
+        picked1_words = gather("picked1_words", words1, list1, J, U16)
+        dy_mx = quantise("dy", interleave("dy_bf", dy_raw))
         w2_mx = quantise("w2", interleave("w2_bf", w2_raw))
         b_acc = product("b_acc", w2_mx, picked2, FP4X4)
-        picked1 = (gather("picked1_words", words1, list1, J, U16), gather("picked1_plane", plane1, list1, J, U8))
+        wo_mx = quantise("wo", interleave("wo_bf", wo_raw))
+        c_acc = product("c_acc", wo_mx, dy_mx, FP8X4)
+        picked1 = (picked1_words, gather("picked1_plane", plane1, list1, J, U8))
+        w1_mx = quantise("w1", interleave("w1_bf", w1_raw), "plane1")
+        a_acc = product("a_acc", w1_mx, picked1, FP4X4)
         gate = new("gate", [P, J], F32)
         nc.scalar.activation(gate[:], b_acc[:], ACT.Sigmoid)
-        wo_mx = quantise("wo", interleave("wo_bf", wo_raw))
-        dy_mx = quantise("dy", interleave("dy_bf", dy_raw))
-        c_acc = product("c_acc", wo_mx, dy_mx, FP8X4)
-        w1_mx = quantise("w1", interleave("w1_bf", w1_raw))
-        a_acc = product("a_acc", w1_mx, picked1, FP4X4)
         gate_picked = gather("gate_picked", gate, list3, M, F32)
-        c_gain = new("c_gain", [P, M], F32)
-        nc.scalar.activation(c_gain[:], c_acc[:], ACT.Copy, scale=gain_col[:])
-        nc.vector.tensor_tensor(placed[:].indirect(list2[:]), gate_picked[:], c_gain[:], ALU.mult)
+        c_neg = new("c_neg", [P, M], F32)
+        nc.scalar.activation(c_neg[:], c_acc[:], ACT.Copy, scale=-1.0)
+        nc.vector.tensor_tensor(placed[:].indirect(list2[:]), gate_picked[:], c_neg[:], ALU.mult)
         hidden = new("hidden", [P, J], F32)
         nc.scalar.activation(hidden[:], a_acc[:], ACT.Tanh)
         squared = new("squared", [P, J], F32)
@@ -135,5 +136,6 @@ def tile_attend_cpickgates_kernel(tc, tab_words, tab_scales, w1, tab2_words, tab
             nc.vector.scalar_tensor_tensor(neg[h][:], squared[:, cols[h]], 1.0, placed[:, cols[h]],
                                            ALU.subtract, ALU.mult)
         for h in range(HALVES):
-            nc.vector.tensor_tensor(res[h][:], old_sb[:, cols[h]], neg[h][:], ALU.subtract)
+            nc.vector.scalar_tensor_tensor(res[h][:], neg[h][:], gain_col[:], old_sb[:, cols[h]],
+                                           ALU.mult, ALU.add)
             nc.sync.dma_start(out[:, cols[h]], res[h][:])

@@ -29,8 +29,8 @@ def tile_attend_cpickgates_kernel(tc, tab_words, tab_scales, w1, tab2_words, tab
         sb = ctx.enter_context(tc.tile_pool(name="sb", bufs=1))
         ps = ctx.enter_context(tc.psum_pool(name="ps", bufs=1))
 
-        def new(name, shape, dtype, tag=None):
-            return sb.tile(shape, dtype, name=name, tag=tag or name, align_bytes=64)
+        def new(name, shape, dtype):
+            return sb.tile(shape, dtype, name=name, align_bytes=64)
 
         def load_list(name, src):
             t = new(name, list(src.shape), U16)
@@ -42,19 +42,26 @@ def tile_attend_cpickgates_kernel(tc, tab_words, tab_scales, w1, tab2_words, tab
             nc.sync.dma_start(t[:].bitcast(I32), src[0].bitcast(I32))
             return t
 
-        def zeroed_plane(name):
-            t = new(name, [P, T], U8)
+        def zeroed_plane(name, width):
+            t = new(name, [P, width], U8)
             nc.vector.memset(t[:].bitcast(I32), 0)
             return t
 
-        def load_scales(t, src):
+        def load_scales(t, src, first):
+            nc.sync.dma_start(t[first:P:8, :].bitcast(I32), src[0].bitcast(I32))
+
+        def load_scales_in_place(t, src):
             rows = src[0].bitcast(I32).rearrange("(q r) c -> r q c", r=4)
             for r in range(4):
                 nc.sync.dma_start(t[r:P:32, :].bitcast(I32), rows[r])
 
-        def load_rows(name, src):
+        def place_scales(queue, plane, picked, first):
+            for r in range(4):
+                queue.dma_start(plane[r:P:32, :].bitcast(I32), picked[first + 8 * r:P:32, :].bitcast(I32))
+
+        def load_rows(name, src, queue=nc.sync):
             t = new(name, [P, PACK, src.shape[1]], F32)
-            nc.sync.dma_start(t[:], src.rearrange("(p t) c -> p t c", t=PACK))
+            queue.dma_start(t[:], src.rearrange("(p t) c -> p t c", t=PACK))
             return t
 
         def interleave(name, raw):
@@ -64,9 +71,9 @@ def tile_attend_cpickgates_kernel(tc, tab_words, tab_scales, w1, tab2_words, tab
                            raw[:].rearrange("p t (c i) -> p c t i", i=LINE))
             return t
 
-        def quantise(name, grouped, tag=None):
+        def quantise(name, grouped):
             width = grouped.shape[1] // PACK
-            codes = new(name + "_codes", [P, width], U32, tag)
+            codes = new(name + "_codes", [P, width], U32)
             plane = new(name + "_plane", [P, width], U8)
             nc.vector.quantize_mx(codes[:].bitcast(FP8X4), plane[:], grouped[:])
             return codes, plane
@@ -82,54 +89,56 @@ def tile_attend_cpickgates_kernel(tc, tab_words, tab_scales, w1, tab2_words, tab
                                 rhs=rhs[0][:].bitcast(rhs_dtype), rhs_scale=rhs[1][:], start=True, stop=True)
             return acc
 
-        plane2 = zeroed_plane("plane2")
-        plane1 = zeroed_plane("plane1")
+        rows2 = zeroed_plane("rows2", T)
+        rows1 = zeroed_plane("rows1", T)
         placed = new("placed", [P, J], F32)
         nc.vector.memset(placed[:], 0.0)
-
+        plane1 = zeroed_plane("plane1", J)
         warm = new("warm", [P, 1], F32)
         nc.scalar.activation(warm[:], placed[:, 0:1], ACT.Sigmoid)
 
         words2 = load_words("words2", tab2_words)
         list4 = load_list("list4", offs4)
-        load_scales(plane2, tab2_scales)
-        dy_raw = load_rows("dy_raw", dy)
-        words1 = load_words("words1", tab_words)
-        list1 = load_list("list1", offs)
+        load_scales_in_place(rows2, tab2_scales)
         w2_raw = load_rows("w2_raw", w2)
+        dy_raw = load_rows("dy_raw", dy)
+        list1 = load_list("list1", offs)
+        load_scales(rows1, tab_scales, 4)
+        words1 = load_words("words1", tab_words)
         wo_raw = load_rows("wo_raw", wo)
         w1_raw = load_rows("w1_raw", w1)
-        load_scales(plane1, tab_scales)
         list3 = load_list("list3", offs3)
         list2 = load_list("list2", offs2)
+
+        picked2 = (gather("picked_words2", words2, list4, J, U16), gather("plane2", rows2, list4, J, U8))
+        w2_mx = quantise("w2", interleave("w2_bf", w2_raw))
+        b_acc = product("b_acc", w2_mx, picked2, FP4X4)
+        picked_rows1 = gather("picked_rows1", rows1, list1, J, U8)
+        place_scales(nc.sync, plane1, picked_rows1, 4)
         gain_col = new("gain_col", [P, 1], F32)
         nc.sync.dma_start(gain_col[:], gain)
         old_sb = new("old_sb", [P, J], F32)
         nc.sync.dma_start(old_sb[:], old)
-
-        picked2 = (gather("picked2_words", words2, list4, J, U16), gather("picked2_plane", plane2, list4, J, U8))
-        picked1_words = gather("picked1_words", words1, list1, J, U16)
         dy_mx = quantise("dy", interleave("dy_bf", dy_raw))
-        w2_mx = quantise("w2", interleave("w2_bf", w2_raw))
-        b_acc = product("b_acc", w2_mx, picked2, FP4X4)
-        wo_mx = quantise("wo", interleave("wo_bf", wo_raw))
-        c_acc = product("c_acc", wo_mx, dy_mx, FP8X4)
-        picked1 = (picked1_words, gather("picked1_plane", plane1, list1, J, U8))
-        w1_mx = quantise("w1", interleave("w1_bf", w1_raw), "plane1")
-        a_acc = product("a_acc", w1_mx, picked1, FP4X4)
         gate = new("gate", [P, J], F32)
         nc.scalar.activation(gate[:], b_acc[:], ACT.Sigmoid)
+        picked1 = (gather("picked_words1", words1, list1, J, U16), plane1)
+        wo_mx = quantise("wo", interleave("wo_bf", wo_raw))
+        c_acc = product("c_acc", wo_mx, dy_mx, FP8X4)
         gate_picked = gather("gate_picked", gate, list3, M, F32)
+        w1_mx = quantise("w1", interleave("w1_bf", w1_raw))
+        a_acc = product("a_acc", w1_mx, picked1, FP4X4)
         c_neg = new("c_neg", [P, M], F32)
         nc.scalar.activation(c_neg[:], c_acc[:], ACT.Copy, scale=-1.0)
         nc.vector.tensor_tensor(placed[:].indirect(list2[:]), gate_picked[:], c_neg[:], ALU.mult)
-        hidden = new("hidden", [P, J], F32)
-        nc.scalar.activation(hidden[:], a_acc[:], ACT.Tanh)
-        squared = new("squared", [P, J], F32)
-        nc.scalar.activation(squared[:], hidden[:], ACT.Square)
-
         width = J // HALVES
         cols = [slice(h * width, (h + 1) * width) for h in range(HALVES)]
+        hidden = new("hidden", [P, J], F32)
+        squared = new("squared", [P, J], F32)
+        for h in range(HALVES):
+            nc.scalar.activation(hidden[:, cols[h]], a_acc[:, cols[h]], ACT.Tanh)
+        for h in range(HALVES):
+            nc.scalar.activation(squared[:, cols[h]], hidden[:, cols[h]], ACT.Square)
         neg = [new("neg%d" % h, [P, width], F32) for h in range(HALVES)]
         res = [new("res%d" % h, [P, width], F32) for h in range(HALVES)]
         for h in range(HALVES):

from contextlib import ExitStack

import concourse.mybir as mybir

K, R, F, T, J, M = 512, 128, 512, 2048, 512, 256
FLOPS = 2 * K * R * J * 2 + 2 * F * R * M

F32 = mybir.dt.float32
BF16 = mybir.dt.bfloat16
I32 = mybir.dt.int32
U32 = mybir.dt.uint32
U16 = mybir.dt.uint16
U8 = mybir.dt.uint8
FP8X4 = mybir.dt.float8_e4m3fn_x4
FP4X4 = mybir.dt.float4_e2m1fn_x4
ACT = mybir.ActivationFunctionType
ALU = mybir.AluOpType

P = 128
PACK = 4
LINE = 4
HALVES = 2


def tile_attend_cpickgates_kernel(tc, tab_words, tab_scales, w1, tab2_words, tab2_scales, w2, gain, wo, dy, old,
                                   offs, offs4, offs2, offs3, out):
    nc = tc.nc
    with ExitStack() as ctx:
        sb = ctx.enter_context(tc.tile_pool(name="sb", bufs=1))
        ps = ctx.enter_context(tc.psum_pool(name="ps", bufs=1))

        def new(name, shape, dtype):
            return sb.tile(shape, dtype, name=name, align_bytes=64)

        def load_list(name, src):
            t = new(name, list(src.shape), U16)
            nc.sync.dma_start(t[:], src)
            return t

        def load_words(name, src):
            t = new(name, [P, T], U16)
            nc.sync.dma_start(t[:].bitcast(I32), src[0].bitcast(I32))
            return t

        def zeroed_plane(name, width):
            t = new(name, [P, width], U8)
            nc.vector.memset(t[:].bitcast(I32), 0)
            return t

        def load_scales(t, src, first):
            nc.sync.dma_start(t[first:P:8, :].bitcast(I32), src[0].bitcast(I32))

        def load_scales_in_place(t, src):
            rows = src[0].bitcast(I32).rearrange("(q r) c -> r q c", r=4)
            for r in range(4):
                nc.sync.dma_start(t[r:P:32, :].bitcast(I32), rows[r])

        def place_scales(queue, plane, picked, first):
            for r in range(4):
                queue.dma_start(plane[r:P:32, :].bitcast(I32), picked[first + 8 * r:P:32, :].bitcast(I32))

        def load_rows(name, src, queue=nc.sync):
            t = new(name, [P, PACK, src.shape[1]], F32)
            queue.dma_start(t[:], src.rearrange("(p t) c -> p t c", t=PACK))
            return t

        def interleave(name, raw):
            width = raw.shape[2]
            t = new(name, [P, width * PACK], BF16)
            nc.scalar.copy(t[:].rearrange("p (c i t) -> p c t i", i=LINE, t=PACK),
                           raw[:].rearrange("p t (c i) -> p c t i", i=LINE))
            return t

        def quantise(name, grouped):
            width = grouped.shape[1] // PACK
            codes = new(name + "_codes", [P, width], U32)
            plane = new(name + "_plane", [P, width], U8)
            nc.vector.quantize_mx(codes[:].bitcast(FP8X4), plane[:], grouped[:])
            return codes, plane

        def gather(name, window, offsets, count, dtype):
            t = new(name, [P, count], dtype)
            nc.vector.tensor_copy(t[:], window[:].indirect(offsets[:]))
            return t

        def product(name, lhs, rhs, rhs_dtype):
            acc = ps.tile([P, rhs[0].shape[1]], F32, name=name)
            nc.tensor.matmul_mx(acc[:], lhsT=lhs[0][:].bitcast(FP8X4), lhsT_scale=lhs[1][:],
                                rhs=rhs[0][:].bitcast(rhs_dtype), rhs_scale=rhs[1][:], start=True, stop=True)
            return acc

        rows2 = zeroed_plane("rows2", T)
        rows1 = zeroed_plane("rows1", T)
        placed = new("placed", [P, J], F32)
        nc.vector.memset(placed[:], 0.0)
        plane1 = zeroed_plane("plane1", J)
        warm = new("warm", [P, 1], F32)
        nc.scalar.activation(warm[:], placed[:, 0:1], ACT.Sigmoid)

        words2 = load_words("words2", tab2_words)
        list4 = load_list("list4", offs4)
        load_scales_in_place(rows2, tab2_scales)
        w2_raw = load_rows("w2_raw", w2)
        dy_raw = load_rows("dy_raw", dy)
        list1 = load_list("list1", offs)
        load_scales(rows1, tab_scales, 4)
        words1 = load_words("words1", tab_words)
        wo_raw = load_rows("wo_raw", wo)
        w1_raw = load_rows("w1_raw", w1)
        list3 = load_list("list3", offs3)
        list2 = load_list("list2", offs2)

        picked2 = (gather("picked_words2", words2, list4, J, U16), gather("plane2", rows2, list4, J, U8))
        w2_mx = quantise("w2", interleave("w2_bf", w2_raw))
        b_acc = product("b_acc", w2_mx, picked2, FP4X4)
        picked_rows1 = gather("picked_rows1", rows1, list1, J, U8)
        place_scales(nc.sync, plane1, picked_rows1, 4)
        gain_col = new("gain_col", [P, 1], F32)
        nc.sync.dma_start(gain_col[:], gain)
        old_sb = new("old_sb", [P, J], F32)
        nc.sync.dma_start(old_sb[:], old)
        dy_mx = quantise("dy", interleave("dy_bf", dy_raw))
        gate = new("gate", [P, J], F32)
        nc.scalar.activation(gate[:], b_acc[:], ACT.Sigmoid)
        picked1 = (gather("picked_words1", words1, list1, J, U16), plane1)
        wo_mx = quantise("wo", interleave("wo_bf", wo_raw))
        c_acc = product("c_acc", wo_mx, dy_mx, FP8X4)
        gate_picked = gather("gate_picked", gate, list3, M, F32)
        w1_mx = quantise("w1", interleave("w1_bf", w1_raw))
        a_acc = product("a_acc", w1_mx, picked1, FP4X4)
        c_neg = new("c_neg", [P, M], F32)
        nc.scalar.activation(c_neg[:], c_acc[:], ACT.Copy, scale=-1.0)
        nc.vector.tensor_tensor(placed[:].indirect(list2[:]), gate_picked[:], c_neg[:], ALU.mult)
        width = J // HALVES
        cols = [slice(h * width, (h + 1) * width) for h in range(HALVES)]
        hidden = new("hidden", [P, J], F32)
        squared = new("squared", [P, J], F32)
        for h in range(HALVES):
            nc.scalar.activation(hidden[:, cols[h]], a_acc[:, cols[h]], ACT.Tanh)
        for h in range(HALVES):
            nc.scalar.activation(squared[:, cols[h]], hidden[:, cols[h]], ACT.Square)
        neg = [new("neg%d" % h, [P, width], F32) for h in range(HALVES)]
        res = [new("res%d" % h, [P, width], F32) for h in range(HALVES)]
        for h in range(HALVES):
            nc.vector.scalar_tensor_tensor(neg[h][:], squared[:, cols[h]], 1.0, placed[:, cols[h]],
                                           ALU.subtract, ALU.mult)
        for h in range(HALVES):
            nc.vector.scalar_tensor_tensor(res[h][:], neg[h][:], gain_col[:], old_sb[:, cols[h]],
                                           ALU.mult, ALU.add)
            nc.sync.dma_start(out[:, cols[h]], res[h][:])
